import numpy as np
import ml_dtypes


def mxq(x, axis, fmt="e4m3"):
    dtype, down = {"e4m3": (ml_dtypes.float8_e4m3fn, 7), "e5m2": (ml_dtypes.float8_e5m2, 14)}[fmt]
    v = np.moveaxis(np.asarray(x, np.float32).astype(ml_dtypes.bfloat16).astype(np.float64), axis, -1)
    blocks = v.reshape(v.shape[:-1] + (-1, 32))
    amax = np.abs(blocks).max(-1, keepdims=True)
    byte = np.maximum(np.where(amax > 0, np.frexp(amax)[1] - 1 + 127, 0) - down, 1)
    scale = np.exp2(byte - 127.0)
    codes = (blocks / scale).astype(np.float32).astype(dtype).astype(np.float64)
    return np.moveaxis((codes * scale).reshape(v.shape), -1, axis)


WIDE = False


def mx_kscale(k):
    if not WIDE:
        return np.ones(k)
    levels = np.array([10, -10, 5, -5, 0])
    if k % 512:
        return np.exp2(np.random.permutation(np.resize(levels, k // 32))).repeat(32)
    a = np.empty((k // 512, 16))
    for p in range(k // 512):
        a[p, :8] = np.random.permutation(np.resize(levels, 8))
        for g in range(8):
            far = levels[np.abs(levels - a[p, g]) >= 10]
            a[p, g + 8] = far[np.random.randint(len(far))]
    return np.exp2(a.ravel()).repeat(32)


def f64(x):
    return np.asarray(x).astype(np.float64)


def striped(idx):
    return np.tile(np.asarray(idx).reshape(-1, 16).T, (8, 1)).astype(np.uint16)


def unstriped(offs):
    return offs[:16].T.reshape(-1).astype(np.int64)


E2M1 = np.array([0.0, 0.5, 1.0, 1.5, 2.0, 3.0, 4.0, 6.0, -0.0, -0.5, -1.0, -1.5, -2.0, -3.0, -4.0, -6.0])


def pack_weight(w, fmt):
    k, n = w.shape
    w = f64(np.asarray(w, np.float32).astype(ml_dtypes.bfloat16)).reshape(k // 32, 32, n)
    amax = np.abs(w).max(1)
    if fmt == "e4m3":
        byte = np.frexp(amax)[1] - 1 + 127 - 7
    else:
        mant, ex = np.frexp(amax / 6.0)
        byte = np.where(mant > 0.5, ex, ex - 1) + 127
    byte = np.clip(np.where(amax > 0, byte, 1), 1, 254)
    scaled = (w * np.exp2(127.0 - byte)[:, None, :]).reshape(k, n).astype(np.float32)
    by_word = np.ascontiguousarray(scaled.reshape(k // 512, 128, 4, n).transpose(0, 1, 3, 2))
    if fmt == "e4m3":
        words = by_word.astype(ml_dtypes.float8_e4m3fn).view(np.uint8)
    else:
        c = by_word.astype(ml_dtypes.float4_e2m1fn).view(np.uint8) & 0xF
        words = (c[..., 0::2] | (c[..., 1::2] << 4)).reshape(k // 512, 128, 2 * n)
    return np.ascontiguousarray(words), np.ascontiguousarray(byte.astype(np.uint8).reshape(k // 512, 16, n))


def unpack_weight(words, scales, fmt):
    g, _, n = scales.shape
    words = np.ascontiguousarray(words).reshape(g, 128, n, -1)
    if fmt == "e4m3":
        vals = words.view(ml_dtypes.float8_e4m3fn).astype(np.float64)
    else:
        nib = np.empty((g, 128, n, 4), np.uint8)
        nib[..., 0::2] = words & 0xF
        nib[..., 1::2] = words >> 4
        vals = E2M1[nib]
    vals = vals * np.repeat(np.exp2(scales.astype(np.float64) - 127.0), 8, axis=1)[..., None]
    return vals.transpose(0, 1, 3, 2).reshape(g * 512, n)


D, T, I, Q, E, K = 512, 2048, 512, 128, 512, 512


def setup_inputs():
    n = np.random.standard_normal
    idx = np.random.permutation(T)[:I]
    fd = mx_kscale(D)
    fk = mx_kscale(K)
    fi = mx_kscale(I)
    ti = np.ones(T)
    ti[idx] = fi
    keysp = pack_weight(n((D, T)) / fd[:, None], "e4m3")
    return {
        "query": (n((D, Q)) * 0.4 / np.sqrt(D) * fd[:, None]).astype(np.float32),
        "query2": (n((K, Q)) * 0.4 / np.sqrt(K) * fk[:, None]).astype(np.float32),
        "keys_words": keysp[0],
        "keys_scales": keysp[1],
        "keys2": (n((K, T)) / fk[:, None]).astype(np.float32),
        "l1": (np.random.uniform(6.2, 6.5, (Q, 1))).astype(np.float32),
        "l2": (np.random.uniform(6.4, 6.7, (Q, 1))).astype(np.float32),
        "size": (np.random.uniform(0.02, 0.08, (1, I)) * fi).astype(np.float32),
        "vals": (n((E, T)) / ti).astype(np.float32),
        "offs": striped(idx),
    }


def reference(query, query2, keys_words, keys_scales, keys2, l1, l2, size, vals, offs):
    idx = unstriped(offs)
    keysu = unpack_weight(keys_words, keys_scales, "e4m3")
    queryq = mxq(f64(query), 0, "e4m3")
    keysidxg = keysu[:, idx]
    a = queryq.T @ keysidxg
    query2q = mxq(f64(query2), 0, "e4m3")
    keys2idxq = mxq(f64(keys2)[:, idx], 0, "e4m3")
    b = query2q.T @ keys2idxq
    r = np.minimum(np.exp(a - f64(l1) - b + f64(l2)), 2.0) * f64(size)
    wt = r.T
    vt = f64(vals)[:, idx].T
    wtq = mxq(wt, 0, "e4m3")
    vtq = mxq(vt, 0, "e4m3")
    o = wtq.T @ vtq
    return o

@@ -1,0 +1,171 @@
+from contextlib import ExitStack
+
+import concourse.mybir as mybir
+from concourse.masks import make_identity
+
+F32 = mybir.dt.float32
+BF16 = mybir.dt.bfloat16
+I32 = mybir.dt.int32
+U32 = mybir.dt.uint32
+U16 = mybir.dt.uint16
+U8 = mybir.dt.uint8
+FP8X4 = mybir.dt.float8_e4m3fn_x4
+ALU = mybir.AluOpType
+ACT = mybir.ActivationFunctionType
+
+P = 128
+PACK = 4
+T, SLOTS, Q, E = 2048, 512, 128, 512
+E_BLOCKS = E // P
+VECTOR_SLOTS = 256
+
+FLOPS = 3 * 2 * 512 * Q * 512
+
+
+def tile_attend_importanceread_kernel(tc, query, query2, keys_words, keys_scales, keys2, l1, l2, size, vals, offs, out):
+    nc = tc.nc
+    with ExitStack() as ctx:
+        sb = ctx.enter_context(tc.tile_pool(name="sb", bufs=1))
+        ps = ctx.enter_context(tc.psum_pool(name="ps", bufs=1))
+        ps2 = ctx.enter_context(tc.psum_pool(name="ps2", bufs=2))
+
+        offsets = sb.tile([P, SLOTS // 16], U16, name="offsets")
+        nc.sync.dma_start(offsets[:], offs)
+
+        key2_rows = keys2.rearrange("(p t) c -> t p c", t=PACK)
+        key2_pool = [sb.tile([P, T], F32, name="key2_pool%d" % t) for t in range(PACK)]
+        val_pool = [sb.tile([P, T], F32, name="val_pool%d" % j, tag="val%d" % j, align_bytes=64) for j in range(E_BLOCKS)]
+        word_pool = sb.tile([P, T], U32, name="word_pool")
+        q_raw = sb.tile([P, PACK, Q], F32, name="q_raw")
+        q2_raw = sb.tile([P, PACK, Q], F32, name="q2_raw")
+        scale_pool = sb.tile([P, T], U8, name="scale_pool")
+        l1_col = sb.tile([P, 1], F32, name="l1_col")
+        l2_col = sb.tile([P, 1], F32, name="l2_col")
+        size_cols = sb.tile([P, PACK], F32, name="size_cols")
+        nc.vector.memset(scale_pool[:].bitcast(I32), 0)
+
+        def load_scales(quad):
+            nc.sync.dma_start(
+                scale_pool[32 * quad : 32 * quad + 4, :].bitcast(I32),
+                keys_scales[0, 4 * quad : 4 * quad + 4, :].bitcast(I32),
+            )
+
+        nc.sync.dma_start(key2_pool[0][:], key2_rows[0])
+        load_scales(0)
+        load_scales(1)
+        nc.sync.dma_start(key2_pool[1][:], key2_rows[1])
+        load_scales(2)
+        load_scales(3)
+        nc.sync.dma_start(q2_raw[:], query2.rearrange("(p t) q -> p t q", t=PACK))
+        nc.sync.dma_start(key2_pool[2][:], key2_rows[2])
+        nc.sync.dma_start(q_raw[:], query.rearrange("(p t) q -> p t q", t=PACK))
+        nc.sync.dma_start(l1_col[:], l1)
+        nc.sync.dma_start(key2_pool[3][:], key2_rows[3])
+        nc.sync.dma_start(l2_col[:], l2)
+        nc.sync.dma_start(size_cols[:], size.rearrange("o (p t) -> (o p) t", t=PACK))
+        nc.sync.dma_start(word_pool[:].bitcast(I32), keys_words[0].rearrange("p c r -> p (c r)").bitcast(I32))
+        for j in range(E_BLOCKS):
+            nc.sync.dma_start(val_pool[j][:], vals[j * P : (j + 1) * P, :])
+
+        ident = sb.tile([P, P], F32, name="ident")
+        make_identity(nc, ident[:])
+
+        key2_bf = sb.tile([P, SLOTS, PACK], BF16, name="key2_bf", align_bytes=64)
+        for t in range(2):
+            nc.vector.tensor_copy(key2_bf[:, :, t], key2_pool[t][:].indirect(offsets[:]))
+
+        q_bf = sb.tile([P, 2, Q, PACK], BF16, name="q_bf", align_bytes=64)
+        nc.scalar.copy(q_bf[:, 1], q2_raw[:].rearrange("p t q -> p q t"))
+        nc.scalar.copy(q_bf[:, 0], q_raw[:].rearrange("p t q -> p q t"))
+        q_codes = sb.tile([P, 2 * Q], U32, name="q_codes", align_bytes=64)
+        q_scales = sb.tile([P, 2 * Q], U8, name="q_scales", align_bytes=64)
+        nc.vector.quantize_mx(q_codes[:].bitcast(FP8X4), q_scales[:], q_bf[:].rearrange("p m q t -> p (m q t)"))
+
+        key_scales = sb.tile([P, SLOTS], U8, name="key_scales", align_bytes=64)
+        nc.vector.tensor_copy(key_scales[:], scale_pool[:].indirect(offsets[:]))
+        log_ratio = sb.tile([P, 1], F32, name="log_ratio")
+        nc.vector.tensor_tensor(log_ratio[:], l2_col[:], l1_col[:], ALU.subtract)
+
+        for t in range(2, PACK):
+            nc.vector.tensor_copy(key2_bf[:, :, t], key2_pool[t][:].indirect(offsets[:]))
+        key2_codes = sb.tile([P, SLOTS], U32, name="key2_codes", align_bytes=64)
+        key2_scales = sb.tile([P, SLOTS], U8, name="key2_scales", align_bytes=64)
+        nc.vector.quantize_mx(key2_codes[:].bitcast(FP8X4), key2_scales[:], key2_bf[:].rearrange("p i t -> p (i t)"))
+        b_ps = ps.tile([P, SLOTS], F32, name="b_ps")
+        nc.tensor.matmul_mx(
+            b_ps[:], lhsT=q_codes[:, Q:].bitcast(FP8X4), lhsT_scale=q_scales[:, Q:],
+            rhs=key2_codes[:].bitcast(FP8X4), rhs_scale=key2_scales[:], start=True, stop=True,
+        )
+        b_dealt = sb.tile([P, PACK, P], F32, name="b_dealt")
+        nc.scalar.copy(b_dealt[:], b_ps[:].rearrange("q (p t) -> q t p", t=PACK))
+
+        key_codes = sb.tile([P, SLOTS], U32, name="key_codes", align_bytes=64)
+        nc.vector.tensor_copy(key_codes[:], word_pool[:].indirect(offsets[:]))
+        a_ps = ps.tile([P, SLOTS], F32, name="a_ps")
+        nc.tensor.matmul_mx(
+            a_ps[:], lhsT=q_codes[:, :Q].bitcast(FP8X4), lhsT_scale=q_scales[:, :Q],
+            rhs=key_codes[:].bitcast(FP8X4), rhs_scale=key_scales[:], start=True, stop=True,
+        )
+        diff = sb.tile([P, PACK, P], F32, name="diff")
+        nc.vector.tensor_tensor(diff[:], a_ps[:].rearrange("q (p t) -> q t p", t=PACK), b_dealt[:], ALU.subtract)
+        ratio = sb.tile([P, PACK, P], F32, name="ratio")
+        nc.scalar.activation(ratio[:], diff[:], ACT.Exp, bias=log_ratio[:])
+        ratio_t = ps.tile([P, PACK, Q], F32, name="ratio_t")
+        for t in range(PACK):
+            nc.tensor.transpose(ratio_t[:, t, :], ratio[:, t, :], ident[:])
+        w_bf = sb.tile([P, Q, PACK], BF16, name="w_bf", align_bytes=64)
+        nc.vector.scalar_tensor_tensor(
+            w_bf[:], ratio_t[:].rearrange("p t q -> p q t"), 2.0,
+            size_cols[:].unsqueeze(1).to_broadcast([P, Q, PACK]), ALU.min, ALU.mult,
+        )
+        w_codes = sb.tile([P, Q], U32, name="w_codes", align_bytes=64)
+        w_scales = sb.tile([P, Q], U8, name="w_scales", align_bytes=64)
+        nc.vector.quantize_mx(w_codes[:].bitcast(FP8X4), w_scales[:], w_bf[:].rearrange("p q t -> p (q t)"))
+
+        cut = VECTOR_SLOTS // 16
+
+        def turn(j, shared):
+            picked = sb.tile([P, SLOTS], BF16, name="picked%d" % j)
+            if shared:
+                nc.vector.tensor_copy(picked[:, :VECTOR_SLOTS], val_pool[j][:].indirect(offsets[:, :cut]))
+                nc.scalar.activation(picked[:, VECTOR_SLOTS:], val_pool[j][:].indirect(offsets[:, cut:]), ACT.Copy)
+            else:
+                nc.scalar.activation(picked[:], val_pool[j][:].indirect(offsets[:]), ACT.Copy)
+            pairs = picked[:].bitcast(F32)
+            turned = ps2.tile([P, 2, P], F32, name="turned")
+            for u in range(2):
+                nc.tensor.transpose(turned[:, u, :], pairs[:, u : SLOTS // 2 : 2], ident[:])
+            return turned[:].rearrange("p u e -> p e u")
+
+        def product(name, v_bf, width, codes_tag):
+            v_codes = sb.tile([P, width], U32, name=name + "_codes", tag=codes_tag, align_bytes=64)
+            v_scales = sb.tile([P, width], U8, name=name + "_scales", align_bytes=64)
+            nc.vector.quantize_mx(v_codes[:].bitcast(FP8X4), v_scales[:], v_bf[:].rearrange("p e t -> p (e t)"))
+            o_ps = ps.tile([P, width], F32, name=name + "_ps")
+            nc.tensor.matmul_mx(
+                o_ps[:], lhsT=w_codes[:].bitcast(FP8X4), lhsT_scale=w_scales[:],
+                rhs=v_codes[:].bitcast(FP8X4), rhs_scale=v_scales[:], start=True, stop=True,
+            )
+            return o_ps
+
+        v01_bf = sb.tile([P, 2 * P, PACK], BF16, name="v01_bf", align_bytes=64)
+        for j in range(2):
+            nc.vector.tensor_copy(v01_bf[:, j * P : (j + 1) * P, :].bitcast(F32), turn(j, False))
+        o01_ps = product("v01", v01_bf, 2 * P, "v01_codes")
+
+        v2_bf = sb.tile([P, P, PACK], BF16, name="v2_bf", align_bytes=64)
+        nc.scalar.copy(v2_bf[:].bitcast(F32), turn(2, True))
+        o01 = sb.tile([P, 2 * P], F32, name="o01", tag="val2", align_bytes=64)
+        nc.vector.tensor_copy(o01[:], o01_ps[:])
+        nc.sync.dma_start(out[:, : 2 * P], o01[:])
+
+        v3_bf = sb.tile([P, P, PACK], BF16, name="v3_bf", align_bytes=64)
+        nc.scalar.copy(v3_bf[:].bitcast(F32), turn(3, True))
+        o2_ps = product("v2", v2_bf, P, "val3")
+        o3_ps = product("v3", v3_bf, P, "v3_codes")
+        o2 = sb.tile([P, P], F32, name="o2")
+        nc.scalar.copy(o2[:], o2_ps[:])
+        nc.sync.dma_start(out[:, 2 * P : 3 * P], o2[:])
+        o3 = sb.tile([P, P], F32, name="o3")
+        nc.vector.tensor_copy(o3[:], o3_ps[:])
+        nc.sync.dma_start(out[:, 3 * P :], o3[:])

@@ -17,7 +17,7 @@ P = 128
 PACK = 4
 T, SLOTS, Q, E = 2048, 512, 128, 512
 E_BLOCKS = E // P
-VECTOR_SLOTS = 256
+VECTOR_SLOTS = 320
 
 FLOPS = 3 * 2 * 512 * Q * 512
 
@@ -26,6 +26,7 @@ def tile_attend_importanceread_kernel(tc, query, query2, keys_words, keys_scales
     nc = tc.nc
     with ExitStack() as ctx:
         sb = ctx.enter_context(tc.tile_pool(name="sb", bufs=1))
+        last = ctx.enter_context(tc.tile_pool(name="last", bufs=1))
         ps = ctx.enter_context(tc.psum_pool(name="ps", bufs=1))
         ps2 = ctx.enter_context(tc.psum_pool(name="ps2", bufs=2))
 
@@ -34,7 +35,8 @@ def tile_attend_importanceread_kernel(tc, query, query2, keys_words, keys_scales
 
         key2_rows = keys2.rearrange("(p t) c -> t p c", t=PACK)
         key2_pool = [sb.tile([P, T], F32, name="key2_pool%d" % t) for t in range(PACK)]
-        val_pool = [sb.tile([P, T], F32, name="val_pool%d" % j, tag="val%d" % j, align_bytes=64) for j in range(E_BLOCKS)]
+        val_pool = [sb.tile([P, T], F32, name="val_pool%d" % j) for j in range(E_BLOCKS - 1)]
+        val_pool.append(last.tile([P, T], F32, name="val_pool_last", align_bytes=64, offset=0))
         word_pool = sb.tile([P, T], U32, name="word_pool")
         q_raw = sb.tile([P, PACK, Q], F32, name="q_raw")
         q2_raw = sb.tile([P, PACK, Q], F32, name="q2_raw")
@@ -75,7 +77,7 @@ def tile_attend_importanceread_kernel(tc, query, query2, keys_words, keys_scales
             nc.vector.tensor_copy(key2_bf[:, :, t], key2_pool[t][:].indirect(offsets[:]))
 
         q_bf = sb.tile([P, 2, Q, PACK], BF16, name="q_bf", align_bytes=64)
-        nc.scalar.copy(q_bf[:, 1], q2_raw[:].rearrange("p t q -> p q t"))
+        nc.scalar.mul(q_bf[:, 1], q2_raw[:].rearrange("p t q -> p q t"), -1.0)
         nc.scalar.copy(q_bf[:, 0], q_raw[:].rearrange("p t q -> p q t"))
         q_codes = sb.tile([P, 2 * Q], U32, name="q_codes", align_bytes=64)
         q_scales = sb.tile([P, 2 * Q], U8, name="q_scales", align_bytes=64)
@@ -91,25 +93,19 @@ def tile_attend_importanceread_kernel(tc, query, query2, keys_words, keys_scales
         key2_codes = sb.tile([P, SLOTS], U32, name="key2_codes", align_bytes=64)
         key2_scales = sb.tile([P, SLOTS], U8, name="key2_scales", align_bytes=64)
         nc.vector.quantize_mx(key2_codes[:].bitcast(FP8X4), key2_scales[:], key2_bf[:].rearrange("p i t -> p (i t)"))
-        b_ps = ps.tile([P, SLOTS], F32, name="b_ps")
+        score = ps.tile([P, SLOTS], F32, name="score")
         nc.tensor.matmul_mx(
-            b_ps[:], lhsT=q_codes[:, Q:].bitcast(FP8X4), lhsT_scale=q_scales[:, Q:],
-            rhs=key2_codes[:].bitcast(FP8X4), rhs_scale=key2_scales[:], start=True, stop=True,
+            score[:], lhsT=q_codes[:, Q:].bitcast(FP8X4), lhsT_scale=q_scales[:, Q:],
+            rhs=key2_codes[:].bitcast(FP8X4), rhs_scale=key2_scales[:], start=True, stop=False,
         )
-        b_dealt = sb.tile([P, PACK, P], F32, name="b_dealt")
-        nc.scalar.copy(b_dealt[:], b_ps[:].rearrange("q (p t) -> q t p", t=PACK))
-
         key_codes = sb.tile([P, SLOTS], U32, name="key_codes", align_bytes=64)
         nc.vector.tensor_copy(key_codes[:], word_pool[:].indirect(offsets[:]))
-        a_ps = ps.tile([P, SLOTS], F32, name="a_ps")
         nc.tensor.matmul_mx(
-            a_ps[:], lhsT=q_codes[:, :Q].bitcast(FP8X4), lhsT_scale=q_scales[:, :Q],
-            rhs=key_codes[:].bitcast(FP8X4), rhs_scale=key_scales[:], start=True, stop=True,
+            score[:], lhsT=q_codes[:, :Q].bitcast(FP8X4), lhsT_scale=q_scales[:, :Q],
+            rhs=key_codes[:].bitcast(FP8X4), rhs_scale=key_scales[:], start=False, stop=True,
         )
-        diff = sb.tile([P, PACK, P], F32, name="diff")
-        nc.vector.tensor_tensor(diff[:], a_ps[:].rearrange("q (p t) -> q t p", t=PACK), b_dealt[:], ALU.subtract)
         ratio = sb.tile([P, PACK, P], F32, name="ratio")
-        nc.scalar.activation(ratio[:], diff[:], ACT.Exp, bias=log_ratio[:])
+        nc.scalar.activation(ratio[:], score[:].rearrange("q (p t) -> q t p", t=PACK), ACT.Exp, bias=log_ratio[:])
         ratio_t = ps.tile([P, PACK, Q], F32, name="ratio_t")
         for t in range(PACK):
             nc.tensor.transpose(ratio_t[:, t, :], ratio[:, t, :], ident[:])
@@ -124,9 +120,9 @@ def tile_attend_importanceread_kernel(tc, query, query2, keys_words, keys_scales
 
         cut = VECTOR_SLOTS // 16
 
-        def turn(j, shared):
+        def turn(j):
             picked = sb.tile([P, SLOTS], BF16, name="picked%d" % j)
-            if shared:
+            if j == E_BLOCKS - 1:
                 nc.vector.tensor_copy(picked[:, :VECTOR_SLOTS], val_pool[j][:].indirect(offsets[:, :cut]))
                 nc.scalar.activation(picked[:, VECTOR_SLOTS:], val_pool[j][:].indirect(offsets[:, cut:]), ACT.Copy)
             else:
@@ -137,35 +133,36 @@ def tile_attend_importanceread_kernel(tc, query, query2, keys_words, keys_scales
                 nc.tensor.transpose(turned[:, u, :], pairs[:, u : SLOTS // 2 : 2], ident[:])
             return turned[:].rearrange("p u e -> p e u")
 
-        def product(name, v_bf, width, codes_tag):
-            v_codes = sb.tile([P, width], U32, name=name + "_codes", tag=codes_tag, align_bytes=64)
-            v_scales = sb.tile([P, width], U8, name=name + "_scales", align_bytes=64)
+        def product(j, v_bf):
+            v_codes = sb.tile([P, P], U32, name="v_codes%d" % j, align_bytes=64)
+            v_scales = sb.tile([P, P], U8, name="v_scales%d" % j, align_bytes=64)
             nc.vector.quantize_mx(v_codes[:].bitcast(FP8X4), v_scales[:], v_bf[:].rearrange("p e t -> p (e t)"))
-            o_ps = ps.tile([P, width], F32, name=name + "_ps")
+            o_ps = ps2.tile([P, P], F32, name="o_ps")
             nc.tensor.matmul_mx(
                 o_ps[:], lhsT=w_codes[:].bitcast(FP8X4), lhsT_scale=w_scales[:],
                 rhs=v_codes[:].bitcast(FP8X4), rhs_scale=v_scales[:], start=True, stop=True,
             )
             return o_ps
 
-        v01_bf = sb.tile([P, 2 * P, PACK], BF16, name="v01_bf", align_bytes=64)
-        for j in range(2):
-            nc.vector.tensor_copy(v01_bf[:, j * P : (j + 1) * P, :].bitcast(F32), turn(j, False))
-        o01_ps = product("v01", v01_bf, 2 * P, "v01_codes")
+        def store(j, result, copy, o_ps):
+            copy(result[:], o_ps[:])
+            nc.sync.dma_start(out[:, j * P : (j + 1) * P], result[:])
 
-        v2_bf = sb.tile([P, P, PACK], BF16, name="v2_bf", align_bytes=64)
-        nc.scalar.copy(v2_bf[:].bitcast(F32), turn(2, True))
-        o01 = sb.tile([P, 2 * P], F32, name="o01", tag="val2", align_bytes=64)
-        nc.vector.tensor_copy(o01[:], o01_ps[:])
-        nc.sync.dma_start(out[:, : 2 * P], o01[:])
+        v_bf = [sb.tile([P, P, PACK], BF16, name="v_bf%d" % j, align_bytes=64) for j in (0, 1, 3)]
+        v_bf.insert(2, last.tile([P, P, PACK], BF16, name="v_bf2", align_bytes=64, offset=0))
+        results = [sb.tile([P, P], F32, name="result%d" % j) for j in (0, 2, 3)]
+        results.insert(1, last.tile([P, P], F32, name="result1", align_bytes=64, offset=1024))
 
-        v3_bf = sb.tile([P, P, PACK], BF16, name="v3_bf", align_bytes=64)
-        nc.scalar.copy(v3_bf[:].bitcast(F32), turn(3, True))
-        o2_ps = product("v2", v2_bf, P, "val3")
-        o3_ps = product("v3", v3_bf, P, "v3_codes")
-        o2 = sb.tile([P, P], F32, name="o2")
-        nc.scalar.copy(o2[:], o2_ps[:])
-        nc.sync.dma_start(out[:, 2 * P : 3 * P], o2[:])
-        o3 = sb.tile([P, P], F32, name="o3")
-        nc.vector.tensor_copy(o3[:], o3_ps[:])
-        nc.sync.dma_start(out[:, 3 * P :], o3[:])
+        nc.vector.tensor_copy(v_bf[0][:].bitcast(F32), turn(0))
+        store(0, results[0], nc.vector.tensor_copy, product(0, v_bf[0]))
+        nc.vector.tensor_copy(v_bf[1][:].bitcast(F32), turn(1))
+        o1 = product(1, v_bf[1])
+        turned2 = turn(2)
+        turned3 = turn(3)
+        store(1, results[1], nc.vector.tensor_copy, o1)
+        nc.vector.tensor_copy(v_bf[2][:].bitcast(F32), turned2)
+        nc.scalar.copy(v_bf[3][:].bitcast(F32), turned3)
+        o2 = product(2, v_bf[2])
+        o3 = product(3, v_bf[3])
+        store(2, results[2], nc.scalar.copy, o2)
+        store(3, results[3], nc.vector.tensor_copy, o3)

@@ -31,20 +31,20 @@ def tile_attend_importanceread_kernel(tc, query, query2, keys_words, keys_scales
         ps2 = ctx.enter_context(tc.psum_pool(name="ps2", bufs=2))
 
         offsets = sb.tile([P, SLOTS // 16], U16, name="offsets")
-        nc.sync.dma_start(offsets[:], offs)
 
         key2_rows = keys2.rearrange("(p t) c -> t p c", t=PACK)
         key2_pool = [sb.tile([P, T], F32, name="key2_pool%d" % t) for t in range(PACK)]
-        val_pool = [sb.tile([P, T], F32, name="val_pool%d" % j) for j in range(E_BLOCKS - 1)]
+        val_pool = [sb.tile([P, T], F32, name="val_pool%d" % j, tag="val%d" % j, align_bytes=64) for j in range(E_BLOCKS - 1)]
         val_pool.append(last.tile([P, T], F32, name="val_pool_last", align_bytes=64, offset=0))
         word_pool = sb.tile([P, T], U32, name="word_pool")
         q_raw = sb.tile([P, PACK, Q], F32, name="q_raw")
         q2_raw = sb.tile([P, PACK, Q], F32, name="q2_raw")
         scale_pool = sb.tile([P, T], U8, name="scale_pool")
-        l1_col = sb.tile([P, 1], F32, name="l1_col")
-        l2_col = sb.tile([P, 1], F32, name="l2_col")
-        size_cols = sb.tile([P, PACK], F32, name="size_cols")
+        l_rows = sb.tile([P, Q], F32, name="l_rows")
+        size_row = sb.tile([P, SLOTS], F32, name="size_row")
         nc.vector.memset(scale_pool[:].bitcast(I32), 0)
+        nc.vector.memset(l_rows[:], 0.0)
+        nc.vector.memset(size_row[:], 0.0)
 
         def load_scales(quad):
             nc.sync.dma_start(
@@ -53,6 +53,7 @@ def tile_attend_importanceread_kernel(tc, query, query2, keys_words, keys_scales
             )
 
         nc.sync.dma_start(key2_pool[0][:], key2_rows[0])
+        nc.sync.dma_start(offsets[:], offs)
         load_scales(0)
         load_scales(1)
         nc.sync.dma_start(key2_pool[1][:], key2_rows[1])
@@ -61,10 +62,10 @@ def tile_attend_importanceread_kernel(tc, query, query2, keys_words, keys_scales
         nc.sync.dma_start(q2_raw[:], query2.rearrange("(p t) q -> p t q", t=PACK))
         nc.sync.dma_start(key2_pool[2][:], key2_rows[2])
         nc.sync.dma_start(q_raw[:], query.rearrange("(p t) q -> p t q", t=PACK))
-        nc.sync.dma_start(l1_col[:], l1)
+        nc.sync.dma_start(l_rows[0:1, :], l1.rearrange("q o -> o q"))
         nc.sync.dma_start(key2_pool[3][:], key2_rows[3])
-        nc.sync.dma_start(l2_col[:], l2)
-        nc.sync.dma_start(size_cols[:], size.rearrange("o (p t) -> (o p) t", t=PACK))
+        nc.sync.dma_start(l_rows[1:2, :], l2.rearrange("q o -> o q"))
+        nc.sync.dma_start(size_row[0:1, :], size)
         nc.sync.dma_start(word_pool[:].bitcast(I32), keys_words[0].rearrange("p c r -> p (c r)").bitcast(I32))
         for j in range(E_BLOCKS):
             nc.sync.dma_start(val_pool[j][:], vals[j * P : (j + 1) * P, :])
@@ -86,7 +87,16 @@ def tile_attend_importanceread_kernel(tc, query, query2, keys_words, keys_scales
         key_scales = sb.tile([P, SLOTS], U8, name="key_scales", align_bytes=64)
         nc.vector.tensor_copy(key_scales[:], scale_pool[:].indirect(offsets[:]))
         log_ratio = sb.tile([P, 1], F32, name="log_ratio")
-        nc.vector.tensor_tensor(log_ratio[:], l2_col[:], l1_col[:], ALU.subtract)
+        l_ps = ps.tile([P, P], F32, name="l_ps")
+        nc.tensor.transpose(l_ps[:], l_rows[:], ident[:])
+        l_cols = sb.tile([P, 2], F32, name="l_cols")
+        nc.scalar.copy(l_cols[:], l_ps[:, 0:2])
+        nc.vector.tensor_tensor(log_ratio[:], l_cols[:, 1:2], l_cols[:, 0:1], ALU.subtract)
+        size_ps = ps.tile([P, PACK, P], F32, name="size_ps")
+        for t in range(PACK):
+            nc.tensor.transpose(size_ps[:, t, :], size_row[:, t::PACK], ident[:])
+        size_cols = sb.tile([P, PACK], F32, name="size_cols")
+        nc.scalar.copy(size_cols[:], size_ps[:, :, 0])
 
         for t in range(2, PACK):
             nc.vector.tensor_copy(key2_bf[:, :, t], key2_pool[t][:].indirect(offsets[:]))
@@ -109,15 +119,6 @@ def tile_attend_importanceread_kernel(tc, query, query2, keys_words, keys_scales
         ratio_t = ps.tile([P, PACK, Q], F32, name="ratio_t")
         for t in range(PACK):
             nc.tensor.transpose(ratio_t[:, t, :], ratio[:, t, :], ident[:])
-        w_bf = sb.tile([P, Q, PACK], BF16, name="w_bf", align_bytes=64)
-        nc.vector.scalar_tensor_tensor(
-            w_bf[:], ratio_t[:].rearrange("p t q -> p q t"), 2.0,
-            size_cols[:].unsqueeze(1).to_broadcast([P, Q, PACK]), ALU.min, ALU.mult,
-        )
-        w_codes = sb.tile([P, Q], U32, name="w_codes", align_bytes=64)
-        w_scales = sb.tile([P, Q], U8, name="w_scales", align_bytes=64)
-        nc.vector.quantize_mx(w_codes[:].bitcast(FP8X4), w_scales[:], w_bf[:].rearrange("p q t -> p (q t)"))
-
         cut = VECTOR_SLOTS // 16
 
         def turn(j):
@@ -125,6 +126,8 @@ def tile_attend_importanceread_kernel(tc, query, query2, keys_words, keys_scales
             if j == E_BLOCKS - 1:
                 nc.vector.tensor_copy(picked[:, :VECTOR_SLOTS], val_pool[j][:].indirect(offsets[:, :cut]))
                 nc.scalar.activation(picked[:, VECTOR_SLOTS:], val_pool[j][:].indirect(offsets[:, cut:]), ACT.Copy)
+            elif j == 0:
+                nc.vector.tensor_copy(picked[:], val_pool[j][:].indirect(offsets[:]))
             else:
                 nc.scalar.activation(picked[:], val_pool[j][:].indirect(offsets[:]), ACT.Copy)
             pairs = picked[:].bitcast(F32)
@@ -132,6 +135,16 @@ def tile_attend_importanceread_kernel(tc, query, query2, keys_words, keys_scales
             for u in range(2):
                 nc.tensor.transpose(turned[:, u, :], pairs[:, u : SLOTS // 2 : 2], ident[:])
             return turned[:].rearrange("p u e -> p e u")
+
+        turned0 = turn(0)
+        w_bf = sb.tile([P, Q, PACK], BF16, name="w_bf", tag="val0", align_bytes=64)
+        nc.vector.scalar_tensor_tensor(
+            w_bf[:], ratio_t[:].rearrange("p t q -> p q t"), 2.0,
+            size_cols[:].unsqueeze(1).to_broadcast([P, Q, PACK]), ALU.min, ALU.mult,
+        )
+        w_codes = sb.tile([P, Q], U32, name="w_codes", align_bytes=64)
+        w_scales = sb.tile([P, Q], U8, name="w_scales", align_bytes=64)
+        nc.vector.quantize_mx(w_codes[:].bitcast(FP8X4), w_scales[:], w_bf[:].rearrange("p q t -> p (q t)"))
 
         def product(j, v_bf):
             v_codes = sb.tile([P, P], U32, name="v_codes%d" % j, align_bytes=64)
@@ -153,7 +166,7 @@ def tile_attend_importanceread_kernel(tc, query, query2, keys_words, keys_scales
         results = [sb.tile([P, P], F32, name="result%d" % j) for j in (0, 2, 3)]
         results.insert(1, last.tile([P, P], F32, name="result1", align_bytes=64, offset=1024))
 
-        nc.vector.tensor_copy(v_bf[0][:].bitcast(F32), turn(0))
+        nc.vector.tensor_copy(v_bf[0][:].bitcast(F32), turned0)
         store(0, results[0], nc.vector.tensor_copy, product(0, v_bf[0]))
         nc.vector.tensor_copy(v_bf[1][:].bitcast(F32), turn(1))
         o1 = product(1, v_bf[1])

@@ -15,9 +15,11 @@ ACT = mybir.ActivationFunctionType
 
 P = 128
 PACK = 4
-T, SLOTS, Q, E = 2048, 512, 128, 512
+QUAD = 32
+TOKENS, SLOTS, Q, E = 2048, 512, 128, 512
 E_BLOCKS = E // P
-VECTOR_SLOTS = 320
+LAST = E_BLOCKS - 1
+VECTOR_SLOTS = 256
 
 FLOPS = 3 * 2 * 512 * Q * 512
 
@@ -31,15 +33,14 @@ def tile_attend_importanceread_kernel(tc, query, query2, keys_words, keys_scales
         ps2 = ctx.enter_context(tc.psum_pool(name="ps2", bufs=2))
 
         offsets = sb.tile([P, SLOTS // 16], U16, name="offsets")
-
         key2_rows = keys2.rearrange("(p t) c -> t p c", t=PACK)
-        key2_pool = [sb.tile([P, T], F32, name="key2_pool%d" % t) for t in range(PACK)]
-        val_pool = [sb.tile([P, T], F32, name="val_pool%d" % j, tag="val%d" % j, align_bytes=64) for j in range(E_BLOCKS - 1)]
-        val_pool.append(last.tile([P, T], F32, name="val_pool_last", align_bytes=64, offset=0))
-        word_pool = sb.tile([P, T], U32, name="word_pool")
+        key2_pool = [sb.tile([P, TOKENS], F32, name="key2_pool%d" % t) for t in range(PACK)]
+        val_pool = [sb.tile([P, TOKENS], F32, name="val_pool%d" % j, tag="val%d" % j, align_bytes=64) for j in range(LAST)]
+        val_pool.append(last.tile([P, TOKENS], F32, name="val_pool_last", align_bytes=64, offset=0))
+        word_pool = sb.tile([P, TOKENS], U32, name="word_pool")
         q_raw = sb.tile([P, PACK, Q], F32, name="q_raw")
         q2_raw = sb.tile([P, PACK, Q], F32, name="q2_raw")
-        scale_pool = sb.tile([P, T], U8, name="scale_pool")
+        scale_pool = sb.tile([P, TOKENS], U8, name="scale_pool")
         l_rows = sb.tile([P, Q], F32, name="l_rows")
         size_row = sb.tile([P, SLOTS], F32, name="size_row")
         nc.vector.memset(scale_pool[:].bitcast(I32), 0)
@@ -48,7 +49,7 @@ def tile_attend_importanceread_kernel(tc, query, query2, keys_words, keys_scales
 
         def load_scales(quad):
             nc.sync.dma_start(
-                scale_pool[32 * quad : 32 * quad + 4, :].bitcast(I32),
+                scale_pool[QUAD * quad : QUAD * quad + 4, :].bitcast(I32),
                 keys_scales[0, 4 * quad : 4 * quad + 4, :].bitcast(I32),
             )
 
@@ -74,7 +75,7 @@ def tile_attend_importanceread_kernel(tc, query, query2, keys_words, keys_scales
         make_identity(nc, ident[:])
 
         key2_bf = sb.tile([P, SLOTS, PACK], BF16, name="key2_bf", align_bytes=64)
-        for t in range(2):
+        for t in range(PACK // 2):
             nc.vector.tensor_copy(key2_bf[:, :, t], key2_pool[t][:].indirect(offsets[:]))
 
         q_bf = sb.tile([P, 2, Q, PACK], BF16, name="q_bf", align_bytes=64)
@@ -86,6 +87,7 @@ def tile_attend_importanceread_kernel(tc, query, query2, keys_words, keys_scales
 
         key_scales = sb.tile([P, SLOTS], U8, name="key_scales", align_bytes=64)
         nc.vector.tensor_copy(key_scales[:], scale_pool[:].indirect(offsets[:]))
+
         log_ratio = sb.tile([P, 1], F32, name="log_ratio")
         l_ps = ps.tile([P, P], F32, name="l_ps")
         nc.tensor.transpose(l_ps[:], l_rows[:], ident[:])
@@ -98,7 +100,7 @@ def tile_attend_importanceread_kernel(tc, query, query2, keys_words, keys_scales
         size_cols = sb.tile([P, PACK], F32, name="size_cols")
         nc.scalar.copy(size_cols[:], size_ps[:, :, 0])
 
-        for t in range(2, PACK):
+        for t in range(PACK // 2, PACK):
             nc.vector.tensor_copy(key2_bf[:, :, t], key2_pool[t][:].indirect(offsets[:]))
         key2_codes = sb.tile([P, SLOTS], U32, name="key2_codes", align_bytes=64)
         key2_scales = sb.tile([P, SLOTS], U8, name="key2_scales", align_bytes=64)
@@ -114,16 +116,17 @@ def tile_attend_importanceread_kernel(tc, query, query2, keys_words, keys_scales
             score[:], lhsT=q_codes[:, :Q].bitcast(FP8X4), lhsT_scale=q_scales[:, :Q],
             rhs=key_codes[:].bitcast(FP8X4), rhs_scale=key_scales[:], start=False, stop=True,
         )
+
         ratio = sb.tile([P, PACK, P], F32, name="ratio")
         nc.scalar.activation(ratio[:], score[:].rearrange("q (p t) -> q t p", t=PACK), ACT.Exp, bias=log_ratio[:])
         ratio_t = ps.tile([P, PACK, Q], F32, name="ratio_t")
         for t in range(PACK):
             nc.tensor.transpose(ratio_t[:, t, :], ratio[:, t, :], ident[:])
-        cut = VECTOR_SLOTS // 16
 
         def turn(j):
             picked = sb.tile([P, SLOTS], BF16, name="picked%d" % j)
-            if j == E_BLOCKS - 1:
+            if j == LAST:
+                cut = VECTOR_SLOTS // 16
                 nc.vector.tensor_copy(picked[:, :VECTOR_SLOTS], val_pool[j][:].indirect(offsets[:, :cut]))
                 nc.scalar.activation(picked[:, VECTOR_SLOTS:], val_pool[j][:].indirect(offsets[:, cut:]), ACT.Copy)
             elif j == 0:
@@ -146,10 +149,10 @@ def tile_attend_importanceread_kernel(tc, query, query2, keys_words, keys_scales
         w_scales = sb.tile([P, Q], U8, name="w_scales", align_bytes=64)
         nc.vector.quantize_mx(w_codes[:].bitcast(FP8X4), w_scales[:], w_bf[:].rearrange("p q t -> p (q t)"))
 
-        def product(j, v_bf):
+        def product(j, block_bf):
             v_codes = sb.tile([P, P], U32, name="v_codes%d" % j, align_bytes=64)
             v_scales = sb.tile([P, P], U8, name="v_scales%d" % j, align_bytes=64)
-            nc.vector.quantize_mx(v_codes[:].bitcast(FP8X4), v_scales[:], v_bf[:].rearrange("p e t -> p (e t)"))
+            nc.vector.quantize_mx(v_codes[:].bitcast(FP8X4), v_scales[:], block_bf[:].rearrange("p e t -> p (e t)"))
             o_ps = ps2.tile([P, P], F32, name="o_ps")
             nc.tensor.matmul_mx(
                 o_ps[:], lhsT=w_codes[:].bitcast(FP8X4), lhsT_scale=w_scales[:],
@@ -157,25 +160,25 @@ def tile_attend_importanceread_kernel(tc, query, query2, keys_words, keys_scales
             )
             return o_ps
 
-        def store(j, result, copy, o_ps):
-            copy(result[:], o_ps[:])
-            nc.sync.dma_start(out[:, j * P : (j + 1) * P], result[:])
+        def store(j, copy, o_ps):
+            copy(results[j][:], o_ps[:])
+            nc.sync.dma_start(out[:, j * P : (j + 1) * P], results[j][:])
 
         v_bf = [sb.tile([P, P, PACK], BF16, name="v_bf%d" % j, align_bytes=64) for j in (0, 1, 3)]
         v_bf.insert(2, last.tile([P, P, PACK], BF16, name="v_bf2", align_bytes=64, offset=0))
         results = [sb.tile([P, P], F32, name="result%d" % j) for j in (0, 2, 3)]
-        results.insert(1, last.tile([P, P], F32, name="result1", align_bytes=64, offset=1024))
+        results.insert(1, last.tile([P, P], F32, name="result1", align_bytes=64, offset=2 * P * PACK))
 
         nc.vector.tensor_copy(v_bf[0][:].bitcast(F32), turned0)
-        store(0, results[0], nc.vector.tensor_copy, product(0, v_bf[0]))
+        store(0, nc.vector.tensor_copy, product(0, v_bf[0]))
         nc.vector.tensor_copy(v_bf[1][:].bitcast(F32), turn(1))
-        o1 = product(1, v_bf[1])
+        o1_ps = product(1, v_bf[1])
         turned2 = turn(2)
         turned3 = turn(3)
-        store(1, results[1], nc.vector.tensor_copy, o1)
-        nc.vector.tensor_copy(v_bf[2][:].bitcast(F32), turned2)
+        store(1, nc.vector.tensor_copy, o1_ps)
+        nc.scalar.copy(v_bf[2][:].bitcast(F32), turned2)
         nc.scalar.copy(v_bf[3][:].bitcast(F32), turned3)
-        o2 = product(2, v_bf[2])
-        o3 = product(3, v_bf[3])
-        store(2, results[2], nc.scalar.copy, o2)
-        store(3, results[3], nc.vector.tensor_copy, o3)
+        o2_ps = product(2, v_bf[2])
+        o3_ps = product(3, v_bf[3])
+        store(2, nc.scalar.copy, o2_ps)
+        store(3, nc.vector.tensor_copy, o3_ps)

from contextlib import ExitStack

import concourse.mybir as mybir
from concourse.masks import make_identity

F32 = mybir.dt.float32
BF16 = mybir.dt.bfloat16
I32 = mybir.dt.int32
U32 = mybir.dt.uint32
U16 = mybir.dt.uint16
U8 = mybir.dt.uint8
FP8X4 = mybir.dt.float8_e4m3fn_x4
ALU = mybir.AluOpType
ACT = mybir.ActivationFunctionType

P = 128
PACK = 4
QUAD = 32
TOKENS, SLOTS, Q, E = 2048, 512, 128, 512
E_BLOCKS = E // P
LAST = E_BLOCKS - 1
VECTOR_SLOTS = 256

FLOPS = 3 * 2 * 512 * Q * 512


def tile_attend_importanceread_kernel(tc, query, query2, keys_words, keys_scales, keys2, l1, l2, size, vals, offs, out):
    nc = tc.nc
    with ExitStack() as ctx:
        sb = ctx.enter_context(tc.tile_pool(name="sb", bufs=1))
        last = ctx.enter_context(tc.tile_pool(name="last", bufs=1))
        ps = ctx.enter_context(tc.psum_pool(name="ps", bufs=1))
        ps2 = ctx.enter_context(tc.psum_pool(name="ps2", bufs=2))

        offsets = sb.tile([P, SLOTS // 16], U16, name="offsets")
        key2_rows = keys2.rearrange("(p t) c -> t p c", t=PACK)
        key2_pool = [sb.tile([P, TOKENS], F32, name="key2_pool%d" % t) for t in range(PACK)]
        val_pool = [sb.tile([P, TOKENS], F32, name="val_pool%d" % j, tag="val%d" % j, align_bytes=64) for j in range(LAST)]
        val_pool.append(last.tile([P, TOKENS], F32, name="val_pool_last", align_bytes=64, offset=0))
        word_pool = sb.tile([P, TOKENS], U32, name="word_pool")
        q_raw = sb.tile([P, PACK, Q], F32, name="q_raw")
        q2_raw = sb.tile([P, PACK, Q], F32, name="q2_raw")
        scale_pool = sb.tile([P, TOKENS], U8, name="scale_pool")
        l_rows = sb.tile([P, Q], F32, name="l_rows")
        size_row = sb.tile([P, SLOTS], F32, name="size_row")
        nc.vector.memset(scale_pool[:].bitcast(I32), 0)
        nc.vector.memset(l_rows[:], 0.0)
        nc.vector.memset(size_row[:], 0.0)

        def load_scales(quad):
            nc.sync.dma_start(
                scale_pool[QUAD * quad : QUAD * quad + 4, :].bitcast(I32),
                keys_scales[0, 4 * quad : 4 * quad + 4, :].bitcast(I32),
            )

        nc.sync.dma_start(key2_pool[0][:], key2_rows[0])
        nc.sync.dma_start(offsets[:], offs)
        load_scales(0)
        load_scales(1)
        nc.sync.dma_start(key2_pool[1][:], key2_rows[1])
        load_scales(2)
        load_scales(3)
        nc.sync.dma_start(q2_raw[:], query2.rearrange("(p t) q -> p t q", t=PACK))
        nc.sync.dma_start(key2_pool[2][:], key2_rows[2])
        nc.sync.dma_start(q_raw[:], query.rearrange("(p t) q -> p t q", t=PACK))
        nc.sync.dma_start(l_rows[0:1, :], l1.rearrange("q o -> o q"))
        nc.sync.dma_start(key2_pool[3][:], key2_rows[3])
        nc.sync.dma_start(l_rows[1:2, :], l2.rearrange("q o -> o q"))
        nc.sync.dma_start(size_row[0:1, :], size)
        nc.sync.dma_start(word_pool[:].bitcast(I32), keys_words[0].rearrange("p c r -> p (c r)").bitcast(I32))
        for j in range(E_BLOCKS):
            nc.sync.dma_start(val_pool[j][:], vals[j * P : (j + 1) * P, :])

        ident = sb.tile([P, P], F32, name="ident")
        make_identity(nc, ident[:])

        key2_bf = sb.tile([P, SLOTS, PACK], BF16, name="key2_bf", align_bytes=64)
        for t in range(PACK // 2):
            nc.vector.tensor_copy(key2_bf[:, :, t], key2_pool[t][:].indirect(offsets[:]))

        q_bf = sb.tile([P, 2, Q, PACK], BF16, name="q_bf", align_bytes=64)
        nc.scalar.mul(q_bf[:, 1], q2_raw[:].rearrange("p t q -> p q t"), -1.0)
        nc.scalar.copy(q_bf[:, 0], q_raw[:].rearrange("p t q -> p q t"))
        q_codes = sb.tile([P, 2 * Q], U32, name="q_codes", align_bytes=64)
        q_scales = sb.tile([P, 2 * Q], U8, name="q_scales", align_bytes=64)
        nc.vector.quantize_mx(q_codes[:].bitcast(FP8X4), q_scales[:], q_bf[:].rearrange("p m q t -> p (m q t)"))

        key_scales = sb.tile([P, SLOTS], U8, name="key_scales", align_bytes=64)
        nc.vector.tensor_copy(key_scales[:], scale_pool[:].indirect(offsets[:]))

        log_ratio = sb.tile([P, 1], F32, name="log_ratio")
        l_ps = ps.tile([P, P], F32, name="l_ps")
        nc.tensor.transpose(l_ps[:], l_rows[:], ident[:])
        l_cols = sb.tile([P, 2], F32, name="l_cols")
        nc.scalar.copy(l_cols[:], l_ps[:, 0:2])
        nc.vector.tensor_tensor(log_ratio[:], l_cols[:, 1:2], l_cols[:, 0:1], ALU.subtract)
        size_ps = ps.tile([P, PACK, P], F32, name="size_ps")
        for t in range(PACK):
            nc.tensor.transpose(size_ps[:, t, :], size_row[:, t::PACK], ident[:])
        size_cols = sb.tile([P, PACK], F32, name="size_cols")
        nc.scalar.copy(size_cols[:], size_ps[:, :, 0])

        for t in range(PACK // 2, PACK):
            nc.vector.tensor_copy(key2_bf[:, :, t], key2_pool[t][:].indirect(offsets[:]))
        key2_codes = sb.tile([P, SLOTS], U32, name="key2_codes", align_bytes=64)
        key2_scales = sb.tile([P, SLOTS], U8, name="key2_scales", align_bytes=64)
        nc.vector.quantize_mx(key2_codes[:].bitcast(FP8X4), key2_scales[:], key2_bf[:].rearrange("p i t -> p (i t)"))
        score = ps.tile([P, SLOTS], F32, name="score")
        nc.tensor.matmul_mx(
            score[:], lhsT=q_codes[:, Q:].bitcast(FP8X4), lhsT_scale=q_scales[:, Q:],
            rhs=key2_codes[:].bitcast(FP8X4), rhs_scale=key2_scales[:], start=True, stop=False,
        )
        key_codes = sb.tile([P, SLOTS], U32, name="key_codes", align_bytes=64)
        nc.vector.tensor_copy(key_codes[:], word_pool[:].indirect(offsets[:]))
        nc.tensor.matmul_mx(
            score[:], lhsT=q_codes[:, :Q].bitcast(FP8X4), lhsT_scale=q_scales[:, :Q],
            rhs=key_codes[:].bitcast(FP8X4), rhs_scale=key_scales[:], start=False, stop=True,
        )

        ratio = sb.tile([P, PACK, P], F32, name="ratio")
        nc.scalar.activation(ratio[:], score[:].rearrange("q (p t) -> q t p", t=PACK), ACT.Exp, bias=log_ratio[:])
        ratio_t = ps.tile([P, PACK, Q], F32, name="ratio_t")
        for t in range(PACK):
            nc.tensor.transpose(ratio_t[:, t, :], ratio[:, t, :], ident[:])

        def turn(j):
            picked = sb.tile([P, SLOTS], BF16, name="picked%d" % j)
            if j == LAST:
                cut = VECTOR_SLOTS // 16
                nc.vector.tensor_copy(picked[:, :VECTOR_SLOTS], val_pool[j][:].indirect(offsets[:, :cut]))
                nc.scalar.activation(picked[:, VECTOR_SLOTS:], val_pool[j][:].indirect(offsets[:, cut:]), ACT.Copy)
            elif j == 0:
                nc.vector.tensor_copy(picked[:], val_pool[j][:].indirect(offsets[:]))
            else:
                nc.scalar.activation(picked[:], val_pool[j][:].indirect(offsets[:]), ACT.Copy)
            pairs = picked[:].bitcast(F32)
            turned = ps2.tile([P, 2, P], F32, name="turned")
            for u in range(2):
                nc.tensor.transpose(turned[:, u, :], pairs[:, u : SLOTS // 2 : 2], ident[:])
            return turned[:].rearrange("p u e -> p e u")

        turned0 = turn(0)
        w_bf = sb.tile([P, Q, PACK], BF16, name="w_bf", tag="val0", align_bytes=64)
        nc.vector.scalar_tensor_tensor(
            w_bf[:], ratio_t[:].rearrange("p t q -> p q t"), 2.0,
            size_cols[:].unsqueeze(1).to_broadcast([P, Q, PACK]), ALU.min, ALU.mult,
        )
        w_codes = sb.tile([P, Q], U32, name="w_codes", align_bytes=64)
        w_scales = sb.tile([P, Q], U8, name="w_scales", align_bytes=64)
        nc.vector.quantize_mx(w_codes[:].bitcast(FP8X4), w_scales[:], w_bf[:].rearrange("p q t -> p (q t)"))

        def product(j, block_bf):
            v_codes = sb.tile([P, P], U32, name="v_codes%d" % j, align_bytes=64)
            v_scales = sb.tile([P, P], U8, name="v_scales%d" % j, align_bytes=64)
            nc.vector.quantize_mx(v_codes[:].bitcast(FP8X4), v_scales[:], block_bf[:].rearrange("p e t -> p (e t)"))
            o_ps = ps2.tile([P, P], F32, name="o_ps")
            nc.tensor.matmul_mx(
                o_ps[:], lhsT=w_codes[:].bitcast(FP8X4), lhsT_scale=w_scales[:],
                rhs=v_codes[:].bitcast(FP8X4), rhs_scale=v_scales[:], start=True, stop=True,
            )
            return o_ps

        def store(j, copy, o_ps):
            copy(results[j][:], o_ps[:])
            nc.sync.dma_start(out[:, j * P : (j + 1) * P], results[j][:])

        v_bf = [sb.tile([P, P, PACK], BF16, name="v_bf%d" % j, align_bytes=64) for j in (0, 1, 3)]
        v_bf.insert(2, last.tile([P, P, PACK], BF16, name="v_bf2", align_bytes=64, offset=0))
        results = [sb.tile([P, P], F32, name="result%d" % j) for j in (0, 2, 3)]
        results.insert(1, last.tile([P, P], F32, name="result1", align_bytes=64, offset=2 * P * PACK))

        nc.vector.tensor_copy(v_bf[0][:].bitcast(F32), turned0)
        store(0, nc.vector.tensor_copy, product(0, v_bf[0]))
        nc.vector.tensor_copy(v_bf[1][:].bitcast(F32), turn(1))
        o1_ps = product(1, v_bf[1])
        turned2 = turn(2)
        turned3 = turn(3)
        store(1, nc.vector.tensor_copy, o1_ps)
        nc.scalar.copy(v_bf[2][:].bitcast(F32), turned2)
        nc.scalar.copy(v_bf[3][:].bitcast(F32), turned3)
        o2_ps = product(2, v_bf[2])
        o3_ps = product(3, v_bf[3])
        store(2, nc.scalar.copy, o2_ps)
        store(3, nc.vector.tensor_copy, o3_ps)
